import numpy as np, ml_dtypes
CORES = [1,5,17,21,33,37,49,53]
N = 8
import mx_ref
BF = ml_dtypes.bfloat16
def gentries(a):
    return np.ascontiguousarray(a.reshape(8, 16, -1).transpose(0, 2, 1)).reshape(8, -1)
def gtable(e):
    e = np.asarray(e); return np.ascontiguousarray(e.reshape(8, -1, 16).transpose(0, 2, 1)).reshape(128, -1).astype(np.int32)
def gcols(t, e):
    v = np.concatenate([t.reshape(8, 16, -1, 4), np.zeros((8, 16, 1, 4), BF)], axis=2)
    return np.ascontiguousarray(np.stack([v[g][:, e[g]] for g in range(8)])).reshape(128, -1)
def tile(rs):
    return np.stack(rs, axis=2).reshape(128, -1).astype(BF)
def cut(t, i, w=512):
    return t[:, w * i:w * i + w]
def pick(q, e):
    c = np.concatenate([q[0].reshape(128, -1, 4), np.zeros((128, 1, 4), np.uint8)], axis=1); s = np.concatenate([q[1], np.ones((16, 1), np.uint8)], axis=1)
    return (np.ascontiguousarray(c[:, e].reshape(128, -1)), np.ascontiguousarray(s[:, e]))
def join(*qs):
    return (np.concatenate([q[0] for q in qs], axis=1), np.concatenate([q[1] for q in qs], axis=1))
def put(q, e, v):
    c, s = q[0].reshape(128, -1, 4).copy(), q[1].copy(); c[:, e] = v[0].reshape(128, -1, 4); s[:, e] = v[1]
    return (c.reshape(128, -1), s)
def pk(c, s):
    return (np.ascontiguousarray(c), mx_ref.live(s))
def emit(q):
    return q[0], q[1]
def packed(v, rng):
    q = [mx_ref.quantize(np.ascontiguousarray(v[r])) for r in range(N)]
    return np.stack([a for a, b in q]), np.stack([mx_ref.plane(b, rng) for a, b in q])
def values_of_codes():
    e, c = np.zeros((128, 128, 4), np.float32), np.zeros((128, 2, 4), np.uint8)
    e[np.arange(128), np.arange(128), 0] = 1
    c[:127, :, 0] = np.arange(256).reshape(2, 128).T[:127]
    return mx_ref.matmul(mx_ref.quantize(e.reshape(128, 512).astype(BF)), (c.reshape(128, 8), np.full((16, 2), 127, np.uint8))).T.reshape(-1).astype(np.float64)
CODE_VALUE, SCALE_VALUE = values_of_codes(), 2.0 ** (np.arange(256) - 127.0)
def decode(q):
    return (CODE_VALUE[q[0]].reshape(16, 8, -1, 4) * SCALE_VALUE[q[1]][:, None, :, None] + 0.0).reshape(128, -1).astype(np.float32)
def f(rng, *shape):
    return mx_ref.flush((rng.standard_normal(shape, dtype=np.float32) * np.exp2(rng.integers(-2, 3, shape[:-1] + (1,)))).astype(BF))
def wide(rng, *shape, cols=0):
    v = rng.standard_normal(shape, dtype=np.float32) * np.exp2(rng.integers(-12, 13, shape)).astype(np.float32)
    if cols: v *= np.repeat(np.exp2(rng.integers(-cols, cols + 1, shape[:-2] + (1, shape[-1] // 4))) * (rng.random(shape[:-2] + (1, shape[-1] // 4)) > 0.0625), 4, axis=-1).astype(np.float32)
    return mx_ref.flush(v.astype(BF))
C, A, R = 384, 64, 2
def at(v, e):
    return np.take_along_axis(v, e, axis=1)
def bottleneck(s, up):
    c = np.abs(s - at(s, up))
    for i in range(9):
        c, up = np.maximum(c, at(c, up)), at(up, up)
    return c
def big(v):
    v = v.astype(np.float32)
    v[np.abs(v) < np.float32(2.0 ** -16)] = 0
    return v.astype(BF)
def numbers_of(rng):
    return {"x": big(f(rng, N, 128, 4 * C)), "u": np.array(f(rng, N, 128, 512)), "v": np.array(f(rng, N, 128, 512))}
def packed_layer(rng, w):
    c, p = packed(np.ascontiguousarray(w).reshape(N, 128, 2048), rng)
    return {"wc": c, "ws": p}
def weights(rng, still=[]):
    w = big(f(rng, N, 128, 2048)).reshape(N, 8, 16, 4, 8, 16, 4)
    for i in still:
        w[:, :, i] = 0
        w[:, :, :, :, :, i] = 0
    return packed_layer(rng, w)
def trees(rng):
    return rng.integers(0, np.maximum(np.arange(C), 1), (N, 8, C))
def places(rng):
    return np.stack([rng.integers(0, C + A * t, (N, 8, A, 4)) for t in range(R)], axis=2)
def lists_of(up, near):
    return {"pa": np.stack([gtable(up[r]) for r in range(N)]), "nr": np.stack([gtable(near[r].reshape(8, -1)) for r in range(N)])}
def signs(rng):
    return np.stack([rng.permutation(8) % 2 * 2.0 - 1.0 for r in range(N)])
def lost():
    t = np.zeros((128, 32, 4), np.float32)
    t[11, :, 0] = 4080
    t[8, :, 0] = 2.0 ** (11.0 - np.arange(32))
    once = decode(mx_ref.quantize(t.reshape(128, 128).astype(BF)))
    twice = decode(mx_ref.quantize(once.astype(BF)))
    e = np.flatnonzero((once[8, ::4] > 0) & (twice[8, ::4] == 0))
    return t[8, e[0] if len(e) else 16, 0]
def setup_inputs(rng):
    return {**numbers_of(rng), **weights(rng), **lists_of(trees(rng), places(rng))}
def setup_inputs_ties(rng):
    d = numbers_of(rng)
    e = rng.permutation(N)
    x = d["x"].reshape(N, 8, 16, C, 4)
    for r in range(N):
        k = np.zeros(C, int) if r == e[0] else rng.permutation(C) % 3
        a = x[r][:, :8, :3].copy()
        a[:, :, 2] = 0
        x[r][:, :8] = a[:, :, k]
    x[e[1]] = 0
    u = d["u"].reshape(N, 8, 16, 128, 4)
    u[:, :, 8:, ::16] = 0
    return {"x": x.reshape(N, 128, 4 * C), "u": u.reshape(N, 128, 512), "v": d["v"], **weights(rng, range(8)), **lists_of(trees(rng), places(rng))}
def setup_inputs_near(rng):
    d = numbers_of(rng)
    up, near = trees(rng), places(rng)
    x = d["x"].astype(np.float32).reshape(N, 8, 16, C, 4)
    x[:, :, 0] = 0
    x[:, :, 8:] = 0
    u = d["u"].reshape(N, 128, 128, 4)
    u[:, :, ::16] = 0
    o, c, j, half = rng.permutation(N) % 4, signs(rng), np.arange(C), C // 2
    for r in range(N):
        if o[r] == 3:
            up[r] = 0
            s = (j + rng.integers(A // 2, half, (8, 1))) % half
            x[r, :, 10, :, 0] = np.where(j < half, 9, 8) * 2.0 ** -30
        else:
            up[r] *= rng.integers(0, 2, (8, C))
            s = ((j + rng.integers(0, C, (8, 1))) % C + 1) // 2
        if o[r] < 2:
            x[r, :, 0, :, 0] = c[r][:, None]
            for g in rng.permutation(8)[:4]: x[r, g, 0, rng.integers(1, C), 0] *= np.float32(2.0 ** 30)
        b = ((s[:, :, None] >> np.arange(8)) & 1) * np.exp2(np.arange(8) - (23.0 if o[r] < 2 else 27.0))
        x[r, :, 8] = b[:, :, :4]
        x[r, :, 9] = b[:, :, 4:]
        k = 1.0 if o[r] == 0 else 2.0 ** -30
        for h in range(0, 128, 16):
            u[r, h, h, 0] = k
            u[r, h + 8:h + 10, h] = k
            u[r, h + 10, h, 0] = k
    x[:, :, 0, 0] = 0
    x[:, :, 8:, 0] = 0
    return {"x": x.reshape(N, 128, 4 * C).astype(BF), "u": u.reshape(N, 128, 512), "v": d["v"], **weights(rng, [0, 8, 9, 10, 11, 12, 13, 14, 15]), **lists_of(up, near)}
def setup_inputs_chains(rng):
    d = numbers_of(rng)
    up, near = trees(rng), places(rng)
    x = d["x"].astype(np.float32).reshape(N, 8, 16, C, 4)
    x[:, :, 8:] = 0
    u = d["u"].reshape(N, 128, 128, 4)
    u[:, :, ::16] = 0
    j = np.arange(C)
    chain, zig, h = np.maximum(j - 1, 0), 1 - 2 * (j % 2), rng.permutation(8)
    k = np.where(rng.permutation(N) < N // 2, 2.0 ** -30, 1.0)
    small = lost()
    p = int(rng.integers(N))
    for r in range(N):
        o = (r - p) % N
        s = rng.integers(0, 1000, (8, C))
        s[h[0], 0] = 4095
        s[h[1]] = 2048 + zig * ((C - j) // 2)
        s[h[2]] = 2048 + zig * ((j + 1) // 2)
        if o < 2:
            s[h[3]] = np.where(j <= A // 2, 1600 + zig * (599 + j), 1600)
            s[h[3], 0] = 0
        s[h[4]] = np.where(j < C // 2, 7, 3000)
        s[h[6]] = rng.integers(0, 8, C)
        s[h[7]] = 0
        up[r, h[:5]] = chain
        up[r, h[5]] = 0
        up[r, h[6]] = np.minimum(chain, C // 2)
        b = ((s[:, :, None] >> np.arange(12)) & 1) * np.exp2(np.arange(12.0))
        for i in range(3): x[r, :, 8 + i] = b[:, :, 4 * i:4 * i + 4]
        x[r, h[7], 8, 1:, 0] = small
        x[r, h[7], 11, :, 0] = 4080
        near[r, h[7], :, :, 0] = rng.integers(1, C, (R, A))
        near[r, h[7], :, :, 1] = 0
        near[r, h[7], 0, A // 2:] = rng.integers(1, C, (A - A // 2, 4))
        own = h[3] if o == 1 else h[5] if o == 3 else h[7]
        m = rng.permutation(h[:7][h[:7] != own])
        near[r, m[0]] = near[r, m[0], :, :1].copy()
        near[r, m[1]] = near[r, m[1], :, :, :1].copy()
        near[r, m[2]] = 0
        near[r, m[3]] = C - 1
        for t in range(R): near[r, m[4], t] = np.resize(rng.permutation(C + A * t), 4 * A).reshape(A, 4)
        near[r, m[5], 1] = C + rng.integers(0, A, (A, 4))
        for i in range(0, 128, 16): u[r, i + 8:i + 11, i] = k[r]
        if o == 1:
            near[r, h[3], 0] = 0
            near[r, h[3], 0, A // 2 + 1:] = np.arange(2, A // 2 + 1)[:, None] - np.array([1, 0, 1, 0])
        if o == 2:
            x[r, h[5], 8:] = 0
            x[r, h[5], 9, 1:, 0] = 10 * 2.0 ** -32
        if o == 3:
            x[r, h[5], 8:] = 0
            x[r, h[5], 8, 1:, 0] = 9 * 2.0 ** -32
            i = 16 * int(h[5])
            u[r, i + 8, i] = 9 * 2.0 ** -33
            u[r, i + 9:i + 11, i] = 2.0 ** -30
            near[r, h[5], 0, :, 0] = 0
    return {"x": x.reshape(N, 128, 4 * C).astype(BF), "u": u.reshape(N, 128, 512), "v": d["v"], **weights(rng, range(8, 16)), **lists_of(up, near)}
def setup_inputs_huge(rng):
    d = numbers_of(rng)
    up = trees(rng)
    c = np.stack([rng.permutation(C) % 2 * 2.0 - 1.0 for r in range(N)])
    c[rng.permutation(N) < N // 2] = -1
    for r in range(N):
        if (c[r] > 0).any():
            c[r, 1:3] = 1, -1
            e = np.where(c[r] > 0, 2, 1)
            e[:3] = 0, 0, 1
            up[r, rng.permutation(8)[:4]] = e
    x = (0.8 + 0.2 * rng.random((N, 128, C, 4))) * np.where(c < 0, -2.0 ** 30, 0.4 * 2.0 ** 30)[:, None, :, None]
    x[:, :, 0] = 0
    u = d["u"].reshape(N, 128, 128, 4)
    a = 2.0 ** 30 * (1 - 0.125 * rng.random((N, 128, 8, 4))) * signs(rng)[:, None, :, None]
    u[:, :, ::16] = a.astype(np.float32).astype(BF)
    w = np.zeros((N, 128, 4, 128, 4), np.float32)
    i = np.arange(128)
    for b in range(4): w[:, i, b, i, b] = 16
    return {"x": x.astype(np.float32).reshape(N, 128, 4 * C).astype(BF), "u": u.reshape(N, 128, 512), "v": d["v"], **packed_layer(rng, w.astype(BF)), **lists_of(up, places(rng))}
def setup_inputs_spread(rng):
    d = setup_inputs(rng)
    d["x"] = big(wide(rng, N, 128, 4 * C, cols=6))
    return d
def check_inputs(d):
    b = []
    for k in ("x", "u", "v"):
        a = np.abs(d[k].astype(np.float32))
        if not (np.isfinite(a).all() and ((a == 0) | (a >= 2.0 ** -30) & (a <= 2.0 ** 30)).all()): b.append("a value of " + k)
    none, least, most = [emit(mx_ref.quantize(np.full((128, 16), k, np.float32).astype(BF)))[1][0, 0] for k in (0.0, 2.0 ** -30, 2.0 ** 30)]
    for r in range(N):
        if ((d["wc"][r] == 0x7F) | (d["wc"][r] == 0xFF)).any(): b.append("wc: a code that is no number")
        s = mx_ref.live(d["ws"][r])
        if ((s != none) & ((s < least) | (s > most))).any(): b.append("ws: a scale out of range")
        e = gentries(d["pa"][r])
        if ((e < 0) | (e > np.maximum(np.arange(C) - 1, 0))).any(): b.append("pa: a parent out of range")
        e = gentries(d["nr"][r]).reshape(8, R, 4 * A)
        if ((e < 0) | (e >= C + A * np.arange(R)[:, None])).any(): b.append("nr: a near place out of range")
    return b
def reference(x, u, v, wc, ws, pa, nr):
    qu = [mx_ref.quantize(u[r]) for r in range(N)]
    lay = [pk(wc[r], ws[r]) for r in range(N)]
    now = [x[r] for r in range(N)]
    up = [gentries(pa[r]) for r in range(N)]
    near = [gentries(nr[r]).reshape(8, R, A, 4) for r in range(N)]
    for t in range(R):
        n = C + A * t
        sent, s, c = [], [], []
        for r in range(N):
            s.append(mx_ref.matmul(qu[r], mx_ref.quantize(now[r]))[::16])
            c.append(bottleneck(s[r], up[r]))
            sent.append(mx_ref.quantize(gcols(now[r], np.argsort(c[r], axis=1, kind="stable")[:, :A])))
        came = decode(join(*sent)).astype(BF)
        for r in range(N):
            new = np.ascontiguousarray(cut(came, (r - 1) % N, 4 * A))
            k = mx_ref.matmul(qu[r], mx_ref.quantize(new))[::16]
            i = near[r][:, t].reshape(8, 4 * A)
            gap = np.abs(at(s[r], i) - np.repeat(k, 4, axis=1))
            cost = np.maximum(at(c[r], i), gap).reshape(8, A, 4)
            parent = np.take_along_axis(near[r][:, t], np.argmin(cost, axis=2)[:, :, None], axis=2)[:, :, 0]
            price = np.maximum(np.repeat(np.min(cost, axis=2), 4, axis=1), gap)
            all_prices = np.full((8, n, A), np.inf, np.float32)
            for g in range(8): all_prices[g, i[g], np.arange(4 * A) // 4] = price[g]
            moved = np.min(all_prices, axis=2) < c[r]
            up[r] = np.concatenate([np.where(moved, n + np.argmin(all_prices, axis=2), up[r]), parent], axis=1)
            z = np.concatenate([now[r], new], axis=1)
            q = mx_ref.quantize(((z.astype(np.float32) + gcols(z, up[r]).astype(np.float32)) * np.float32(0.5)).astype(BF))
            now[r] = tile([np.maximum(mx_ref.matmul(pick(lay[r], np.arange(128 * b, 128 * b + 128)), q), np.float32(0.0)) * np.float32(0.03125) + z[:, b::4].astype(np.float32) for b in range(4)])
    n = C + A * R
    y, op = np.zeros((N, 128, n), np.float32), np.zeros((N, 8, n), np.float32)
    oc, osc = np.zeros((N, 128, 4 * n), np.uint8), np.zeros((N, 16, n), np.uint8)
    for r in range(N):
        q = mx_ref.quantize(now[r])
        y[r] = mx_ref.matmul(mx_ref.quantize(v[r]), q)
        op[r] = up[r]
        oc[r], osc[r] = emit(q)
    return {"y": y, "op": op, "oc": oc, "osc": osc}

from concourse.mybir import dt, AluOpType as A, AxisListType as AX, ActivationFunctionType as F

C, NEW = 384, 64
BIG = 1.0e29
f32, bf, i32, u16, u8, mx, f16 = "float32", "bfloat16", "int32", "uint16", "uint8", "float8_e4m3fn_x4", "float16"
_B = {
    "xt0": (1792, bf), "xt1": (2048, bf), "xt2": (2048, bf), "xh": (2048, bf), "yt": (2048, bf), "rb": (2048, f32), "dp": (1792, bf),
    "ut": (512, bf), "vt": (512, bf), "qu": (128, mx), "su": (128, u8), "qp": (128, mx), "sp": (128, u8), "qv": (128, mx), "sv": (128, u8),
    "qw": (512, mx), "sw": (512, u8), "qx0": (384, mx), "sx0": (384, u8), "qx1": (448, mx), "sx1": (448, u8), "qx2": (512, mx), "sx2": (512, u8),
    "qi0": (384, mx), "si0": (384, u8), "qi1": (448, mx), "si1": (448, u8), "qh": (128, mx), "sh": (128, u8), "qy": (512, mx), "sy": (512, u8),
    "ct1": (3584, bf), "qc1": (896, mx), "sc1": (896, u8), "ct2": (1536, bf), "qc2": (384, mx), "sc2": (384, u8),
    "et": (2048, bf), "qe": (512, mx), "se": (512, u8), "bd": (2048, bf), "qb": (512, mx), "sb": (512, u8),
    "pai": (24, i32), "nri": (32, i32), "eo0": (4, u16), "eo1": (4, u16), "ei0": (4, u16), "ei1": (4, u16),
    "ip": (8, i32), "im": (32, f32), "rf": (16, f32), "cst": (16, f32), "c16": (96, f32), "iq": (32, f32),
    "co": (96, u16), "cw": (64, f32), "iom": (512, bf), "kd": (512, bf), "mk": (224, f32), "kf": (224, f32), "cr": (256, f32), "tk": (256, bf),
    "k4": (256, f32), "tb": (16, f32),
    "pf": (768, f32), "ta": (448, bf), "tb2": (448, bf), "ds": (512, f16), "lv": (320, u16),
    "s": (896, f32), "ca": (896, f32), "cb": (896, f32), "xg": (2048, bf), "pm": (224, f32), "b1": (224, f32), "h1": (224, f32), "dg": (1344, bf),
    "m1": (224, bf), "px": (224, bf), "pv": (696, bf), "junk": (5216, bf), "jf": (396, f32), "a1": (8, f32), "l2": (8, u16),
    "r2": (128, f32), "b2": (128, f32), "h2": (128, f32), "x2": (128, f32), "w2": (128, f32), "cl": (528, f32), "a2": (4, f32),
    "no": (32, u16), "kw": (32, f32), "kr": (512, f32), "ar": (32, f32), "ro": (32, u16), "sk": (544, f32), "sd": (512, f32), "ki": (320, i32),
    "so": (128, u16), "nf": (256, f32), "dq": (512, f32), "ks": (544, f32), "ak": (512, f32),
    "sn": (256, f32), "de": (256, f32), "ga": (256, f32), "gs": (256, f32), "cs": (256, f32), "dm": (256, f32), "ge": (256, bf),
    "pq": (256, f32), "pi": (128, i32), "pr": (256, f32), "s1": (256, f32), "ne": (256, bf), "mv": (256, bf), "d1": (256, f32), "d2": (256, f32), "s2": (256, f32),
    "yo": (512, f32),
}
SCRATCH = {k: ("sbuf", [128, w], d) for k, (w, d) in _B.items()}
SCRATCH["ps"] = ("psum", [128, 4096], f32)
NS = 140
SEMAPHORES = ["w%d" % i for i in range(NS)] + ["sent", "ax0", "ax1", "ae0", "ae1"]
CY, GA, SC, WAKE = 1.04, 1.56, 3.8, 150.0


def V(b, a, e, s=1):
    return (b, a, e, s)


def G(b, a, e, off):
    return (b, a, e, 1, off)


def _len(v):
    return 16 * _len(v[4]) if len(v) == 5 else len(range(v[1], v[2], v[3]))


def _bits(v):
    if v[0] == "ps":
        return sum(1 << k for k in range(v[1] // 512, (v[2] - 1) // 512 + 1))
    if v[3] == 1:
        return ((1 << (v[2] - v[1])) - 1) << v[1]
    return sum(1 << k for k in range(v[1], v[2], v[3]))


def _two(*vs):
    return all(v[0] != "ps" and _B[v[0]][1] in (bf, f16, u16) for v in vs)


def collect(g, core, T, topo, rank):
    ops = []
    n_ranks = len(T.cores)
    nxt, prv = T.cores[(rank + 1) % n_ranks], T.cores[(rank - 1) % n_ranks]
    rid, pid = topo.addr(nxt)[:2]
    mask = topo.mask(core, nxt)
    n_out, n_in = len(topo.engines(core, nxt)), len(topo.engines(prv, core))

    def ap(v):
        if not isinstance(v, tuple):
            return v
        x = T[v[0]][:, v[1]:v[2]] if v[3] == 1 else T[v[0]][:, v[1]:v[2]:v[3]]
        return x.indirect(ap(v[4])) if len(v) == 5 else x

    def add(q, cost, rd, wr, fn, lat=0.0, kind="c", acc=False, sem=None):
        r = []
        for v in rd + wr:
            if isinstance(v, tuple) and len(v) == 5:
                r.append(v[4])
        r += [v for v in rd if isinstance(v, tuple)]
        ops.append({"q": q, "cost": cost, "lat": lat, "rd": r, "wr": wr, "fn": fn, "kind": kind, "acc": acc, "sem": sem})

    def est(o, i, f):
        if len(o) == 5:
            return 55 + _len(o) * CY * SC
        if len(i) == 5:
            return 55 + _len(i) * CY * GA
        return max(64, _len(o) * f) * CY

    def cp(o, i):
        add("v", est(o, i, 0.5 if _two(o, i) else 1), [i], [o], lambda: g.vector.tensor_copy(ap(o), ap(i)))

    def tt(o, a, b, op):
        add("v", est(o, a, 1 if "ps" in (a[0], b[0]) else 2), [a, b], [o], lambda: g.vector.tensor_tensor(ap(o), ap(a), ap(b), op))

    def ts(o, a, s1, op0, s2=None, op1=None):
        if s2 is None:
            fn = lambda: g.vector.tensor_scalar(ap(o), ap(a), ap(s1), None, op0)
        else:
            fn = lambda: g.vector.tensor_scalar(ap(o), ap(a), ap(s1), ap(s2), op0, op1)
        add("v", est(o, a, 0.5 if _two(o, a) else 1), [a, s1, s2], [o], fn)

    def scan(o, a, b, init, op0, op1):
        add("v", est(o, a, 0.5 if _two(o, a, b) else 1), [a, b], [o], lambda: g.vector.tensor_tensor_scan(ap(o), ap(a), ap(b), init, op0, op1))

    def red(o, a):
        add("v", est(a, a, 1), [a], [o], lambda: g.vector.tensor_reduce(ap(o), ap(a), AX.X, A.add))

    def ms(o, c):
        add("v", est(o, o, 0.5 if _two(o) else 1), [], [o], lambda: g.vector.memset(ap(o), c))

    def act(o, i, f, bias=None, scale=None, acc=None):
        def fn():
            k = {}
            if bias is not None:
                k["bias"] = ap(bias)
            if scale is not None:
                k["scale"] = ap(scale)
            if acc is not None:
                k["accum_out"] = ap(acc)
            return g.scalar.activation(ap(o), ap(i), f, **k)
        add("a", est(o, i, 1) + (20 if acc else 0), [i, bias, scale], [o] + ([acc] if acc else []), fn)

    def qz(q, s, a, e, i):
        add("v", 12 + 0.275 * _len(i), [i], [V(q, a, e), V(s, a, e)], lambda: g.vector.quantize_mx(ap(V(q, a, e)), ap(V(s, a, e)), ap(i)))

    def mm(bank, lq, ls, la, rq, rs, a, e, start=True, stop=True):
        o, l1, l2, r1, r2 = V("ps", 512 * bank, 512 * bank + e - a), V(lq, la, la + 128), V(ls, la, la + 128), V(rq, a, e), V(rs, a, e)
        add("t", (e - a + 16) * 1.07, [l1, l2, r1, r2], [o], lambda: g.tensor.matmul_mx(ap(o), ap(l1), ap(l2), ap(r1), ap(r2), start, stop), acc=not start)

    def iot(o, pat, base, cm):
        if _B[o[0]][1] == i32:
            fn = lambda: g.iota(ap(o), pat, base, cm)
        else:
            fn = lambda: g.iota(ap(o), pat, base, cm, allow_small_or_imprecise_dtypes=True)
        add("g", 150 + 2 * CY * _len(o), [], [o], fn)

    def sel(o, pat, cmp, base, cm):
        add("g", 170 + 2 * CY * _len(o), [o], [o], lambda: g.affine_select(ap(o), ap(o), pat, cmp, 0.0, base, cm))

    def dma(q, o, i, rd, wr, nbytes):
        e = {"s": g.sync, "a": g.scalar}[q]
        add(q, 60, rd, wr, lambda: e.dma_start(o(), i()), lat=1900 + nbytes / 180.0, kind="d")

    def remote(items, sem, nbytes):
        for k, (o, i, codes) in enumerate(items):
            def fn(o=o, i=i, codes=codes):
                a, b = (ap(o).bitcast(dt.uint8), ap(i).bitcast(dt.uint8)) if codes else (ap(o), ap(i))
                return g.remote_dma(a, b, T.sem[sem], T.sem.sent, pid, rid, mask)
            add("g", 300, [i], [("@" + sem, k, k + 1, 1)], fn, kind="r")
        add("n", 0, [("@" + sem, 0, len(items), 1)], [o for o, i, c in items], None, lat=2500 + nbytes / 64.0, kind="n", sem=(sem, n_in * len(items)))

    def col(b, k):
        return V(b, k, k + 1)

    def wrap(o, src, a, n, sub):
        scan(V("ds", 0, n), V("kd", 0, n), V(src, a, a + n), 0.0, A.add, A.max)
        ts(o, V("ds", 15, n, 16), col("cst", sub), A.subtract)

    dma("a", lambda: T.xt0[:, 0:768], lambda: T.x[:, 0:768], [], [V("xt0", 0, 768)], 200000)
    dma("s", lambda: T.pai[:], lambda: T.pa[:], [], [V("pai", 0, 24)], 0)
    dma("s", lambda: T.xt0[:, 768:1536], lambda: T.x[:, 768:1536], [], [V("xt0", 768, 1536)], 400000)
    dma("a", lambda: T.ut[:], lambda: T.u[:], [], [V("ut", 0, 512)], 300000)
    dma("s", lambda: T.nri[:], lambda: T.nr[:], [], [V("nri", 0, 32)], 0)
    dma("s", lambda: T.qw[:].bitcast(dt.uint8), lambda: T.wc[:], [V("xt0", 0, 1536)], [V("qw", 0, 512)], 260000)
    dma("s", lambda: T.sw[:], lambda: T.ws[:], [V("xt0", 0, 1536)], [V("sw", 0, 512)], 260000)
    dma("s", lambda: T.vt[:], lambda: T.v[:], [V("xt0", 0, 1536)], [V("vt", 0, 512)], 260000)

    iot(V("ip", 0, 2), [[0, 2]], 0, 1)
    iot(V("im", 0, 32), [[16, 32]], 0, 0)
    iot(V("rf", 0, 16), [[1, 16]], 0, 0)
    iot(V("iom", 0, 512), [[1, 512]], -256, 0)
    iot(V("cr", 0, 256), [[-1, 256]], 255, 0)
    iot(V("tk", 0, 256), [[1, 64], [0, 4]], 0, 0)
    ts(col("ip", 2), col("ip", 0), 15, A.bitwise_and)
    cp(col("cst", 0), col("ip", 2))
    qf = col("cst", 0)
    ts(col("cst", 1), qf, 15.0, A.is_lt, 512.0, A.mult)
    ts(col("cst", 2), col("cst", 1), 256.0, A.subtract)
    ts(col("ip", 3), col("ip", 0), 1, A.bitwise_and)
    ts(col("cst", 4), col("ip", 3), 192.0, A.add)
    ts(col("cst", 5), col("ip", 3), 224.0, A.add)
    ts(col("ip", 4), col("ip", 2), 1, A.arith_shift_right)
    ts(col("cst", 6), col("ip", 4), 0.5, A.add)
    ts(V("c16", 48, 64), V("rf", 0, 16), qf, A.subtract)
    ts(V("c16", 64, 80), V("c16", 48, 64), 0.0, A.is_equal, -2048.0, A.mult)
    ts(V("c16", 80, 96), V("c16", 48, 64), 1.0, A.is_equal, 512.0, A.mult)
    tt(V("c16", 0, 16), V("c16", 64, 80), V("c16", 80, 96), A.add)
    ts(V("c16", 16, 32), V("c16", 48, 64), 0.0, A.is_le, BIG, A.mult)
    ts(V("c16", 16, 32), V("c16", 16, 32), 1.0, A.subtract)
    ts(V("c16", 32, 48), V("c16", 48, 64), 0.0, A.is_gt, BIG, A.mult)
    ts(V("c16", 32, 48), V("c16", 32, 48), 1.0, A.subtract)
    ts(V("co", 0, 32), V("im", 0, 32), 0.0, A.mult, qf, A.add)
    cp(V("co", 32, 40), V("im", 0, 8))
    ts(V("co", 40, 56), V("im", 0, 16), 15.0, A.add)
    ts(V("iq", 0, 32), V("im", 0, 32), qf, A.add)
    ts(V("cw", 0, 16), V("iq", 0, 16), -1.0 / 256, A.mult, 255.0 / 256 - 256.0, A.add)
    ts(V("cw", 16, 32), V("iq", 0, 16), 512.0, A.add)
    ts(V("cw", 32, 40), V("im", 0, 8), 0.5, A.mult, col("cst", 6), A.add)
    ts(V("cw", 40, 44), V("iq", 0, 4), 32.5, A.subtract)
    ts(V("cw", 44, 48), V("iq", 0, 4), 31.5, A.subtract)
    ts(V("cl", 128, 528, 132), V("iq", 0, 4), -127.0, A.mult, 4096.0 - 63.0, A.add)
    cp(V("kd", 0, 384), G("c16", 0, 16, V("co", 0, 24)))
    act(V("kd", 384, 512), V("kd", 0, 128), F.Copy)
    act(V("mk", 0, 224), G("c16", 16, 32, V("co", 0, 14)), F.Copy)
    act(V("kf", 0, 224), G("c16", 32, 48, V("co", 0, 14)), F.Copy)
    act(V("cr", 0, 256), V("cr", 0, 256), F.Copy, scale=1.0 / 256)
    ms(V("pv", 192, 696, 232), -192.0)
    ms(V("pv", 224, 696, 232), -224.0)
    ms(V("ct1", 2688, 3584), 0.0)
    ms(V("ct2", 1024, 1536), 0.0)
    ms(V("ge", 0, 256, 4), 0.0)
    ms(V("k4", 0, 256), 0.0)
    ms(V("k4", 0, 256, 4), BIG)
    ms(col("tb", 0), 0.0)
    ms(col("tb", 1), BIG)
    ms(V("sk", 256, 544, 272), 255.5)
    ms(V("ks", 0, 544, 272), 0.0)
    iot(V("bd", 0, 512), [[0, 512]], 1, 0)
    sel(V("bd", 0, 512), [[-16, 8], [0, 64]], A.is_ge, 0, 1)
    sel(V("bd", 0, 512), [[16, 8], [0, 64]], A.is_ge, 15, -1)
    act(V("bd", 512, 1024), V("bd", 0, 512), F.Copy, scale=0.5)
    act(V("bd", 1024, 1536), V("bd", 0, 512), F.Copy)
    act(V("bd", 1026, 1536, 4), V("bd", 2, 512, 4), F.Copy, scale=-1.0)
    act(V("bd", 1536, 2048), V("bd", 0, 512), F.Copy)
    act(V("bd", 1536, 2048, 4), V("bd", 0, 512, 4), F.Copy, scale=0.5)
    act(V("bd", 1537, 2048, 4), V("bd", 1, 512, 4), F.Copy, scale=0.5)
    qz("qb", "sb", 0, 512, V("bd", 0, 2048))
    for b in range(4):
        iot(V("et", 512 * b, 512 * b + 512), [[0, 512]], 1, 0)
        sel(V("et", 512 * b, 512 * b + 512), [[-1, 512]], A.is_equal, b, 4)
        qz("qe", "se", 128 * b, 128 * b + 128, V("et", 512 * b, 512 * b + 512))
    qz("qu", "su", 0, 128, V("ut", 0, 512))
    uo = V("co", 32, 40)
    add("v", 260, [V("qu", 0, 128), uo], [V("qp", 0, 128)],
        lambda: g.vector.tensor_copy(T.qp[:, 0:128].bitcast(dt.uint32), T.qu[:, 0:128].bitcast(dt.uint32).indirect(ap(uo))))
    act(V("sp", 0, 128), G("su", 0, 128, uo), F.Copy)
    qz("qv", "sv", 0, 128, V("vt", 0, 512))
    cp(V("no", 0, 32), V("nri", 0, 32))
    cp(V("lv", 0, 24), V("pai", 0, 24))
    act(V("pf", 0, C), G("iom", 0, 512, V("lv", 0, 24)), F.Identity, bias=256.0)
    qz("qx0", "sx0", 0, 192, V("xt0", 0, 768))
    qz("qx0", "sx0", 192, 384, V("xt0", 768, 1536))

    for t in range(2):
        n = C + NEW * t
        M, N = n // 16, n // 2
        xt, xn, qx, sx, qi, si = "xt%d" % t, "xt%d" % (t + 1), "qx%d" % t, "sx%d" % t, "qi%d" % t, "si%d" % t
        lv = lambda i, a=0, e=None: V("lv", 32 * i + a, 32 * i + (M if e is None else e))
        remote([(V(qi, 0, n), V(qx, 0, n), True), (V(si, 0, n), V(sx, 0, n), False)], "ax%d" % t, 640 * n)
        for k in range(4):
            mm(k, "qp", "sp", 0, qx, sx, k // 2 * N, k // 2 * N + N)
        act(V("s", 0, N), V("ps", 0, N), F.Copy)
        act(V("s", 448, 448 + N), V("ps", 512, 512 + N), F.Copy)
        cp(V("s", N, n), V("ps", 1024, 1024 + N))
        act(V("s", 448 + N, 448 + n), V("ps", 1536, 1536 + N), F.Copy)
        for b in range(4):
            mm(b, "qe", "se", 128 * b, qi, si, 0, n)
            act(V("dp", 448 * b, 448 * b + n), V("ps", 512 * b, 512 * b + n), F.Copy)
            act(V("xh", 512 * b, 512 * b + n), V(xt, b, 4 * n, 4), F.Copy, scale=0.5)
            dma("s", lambda b=b, n=n: T.xg[:, 512 * b:512 * b + n], lambda b=b, n=n: T.xh[:, 512 * b:512 * b + n],
                [V("xh", 512 * b, 512 * b + n)], [V("xg", 512 * b, 512 * b + n)], 256 * n)
        o = 16 * t
        no = V("no", o, o + 16)
        kr, sk = V("kr", 256 * t, 256 * t + 256), 272 * t
        tt(V("kw", o, o + 16), V("nri", o, o + 16), V("cw", 0, 16), A.add)
        tt(kr, G("iom", 0, 512, no), V("cr", 0, 256), A.add)
        for m in range(16):
            act(V("junk", 256 * m, 256 * m + 256), kr, F.Sign, bias=col("kw", o + m), scale=-1.0, acc=col("ar", o + m))
        ts(V("ro", o, o + 16), V("ar", o, o + 16), 255.0, A.add, 0.5, A.mult)
        cp(G("sk", sk, sk + 256, V("ro", o, o + 16)), kr)
        scan(V("sd", 0, 256), V("kd", 0, 256), V("sk", sk, sk + 256), 0.0, A.add, A.max)
        scan(V("sd", 256, 512), V("kd", 0, 256), V("sk", sk + 1, sk + 257), 0.0, A.add, A.max)
        ki = lambda k, w=16: V("ki", 160 * t + 16 * k, 160 * t + 16 * k + w)
        so = lambda k: V("so", 64 * t + 16 * k, 64 * t + 16 * k + 16)
        ts(ki(0, 32), V("sd", 15, 512, 16), col("cst", 2), A.subtract, 256.0, A.mult)
        ts(ki(2, 32), ki(0, 32), 8, A.arith_shift_right)
        ts(ki(4), ki(0), 255, A.bitwise_and)
        ts(ki(5), ki(0), 252, A.bitwise_and)
        ts(so(0), ki(4), -1.0, A.mult, 255.0, A.add)
        ts(so(1), ki(5), -1.0, A.mult, 255.0, A.add)
        cp(so(2), ki(2))
        tt(ki(6), ki(2), ki(3), A.not_equal)
        tt(ki(7), ki(2), V("cw", 16, 32), A.subtract)
        tt(ki(8), ki(7), ki(6), A.mult)
        tt(ki(9), ki(8), V("cw", 16, 32), A.add)
        cp(so(3), ki(9))
        eo = V("ro", o, o + 16)
        cp(eo, ki(6))
        ks = 272 * t
        act(V("ks", ks + 1, ks + 257), G("tb", 0, 2, eo), F.Copy)
        ak = V("ak", 256 * t, 256 * t + 256)
        act(ak, G("tk", 0, 256, so(0)), F.Identity, bias=float(n))
        act(V("nf", 0, 256), G("iom", 0, 512, no), F.Copy)
        for a in range(4):
            act(V("dq", 256 * t + a, 256 * t + 256, 4), V("nf", a, 256, 4), F.Identity, bias=256.0 + 512.0 * (3 - a))
        levels = 6 if t == 0 else 8
        tab = ["ta", "tb2"]
        act(V(tab[1], 0, n), G("pf", 0, n, lv(0)), F.Identity, bias=-256.0)
        for i in range(1, levels + 1):
            if i > 1:
                act(V(tab[i % 2], 0, n), G(tab[(i - 1) % 2], 0, n, lv(i - 1)), F.Copy)
            wrap(lv(i), tab[i % 2], 0, n, 2)
        halves = [(0, N), (N, n)]
        for a, e in halves:
            tt(V("cb", a, e), G("s", 0, n, lv(0, a // 16, e // 16)), V("s", 448 + a, 448 + e), A.subtract)
            act(V("ca", a, e), V("cb", a, e), F.Abs)
            act(V("ca", 448 + a, 448 + e), V("cb", a, e), F.Abs)
        cc = ["ca", "cb"]
        steps = 6 if t == 0 else 9
        for i in range(steps):
            for a, e in halves:
                tt(V(cc[(i + 1) % 2], a, e), G(cc[i % 2], 0, n, lv(i, a // 16, e // 16)), V(cc[i % 2], 448 + a, 448 + e), A.max)
                if i < steps - 1:
                    act(V(cc[(i + 1) % 2], 448 + a, 448 + e), V(cc[(i + 1) % 2], a, e), F.Copy)
        c = cc[steps % 2]
        if t == 0:
            for b in range(1, n // 64):
                tt(V(c, 64 * b, 64 * b + 64), G(c, 0, 64 * b, lv(6, 4 * b, 4 * b + 4)), V(c, 64 * b, 64 * b + 64), A.max)
        act(V("sn", 0, 256), G("s", 0, n, no), F.Copy)

        def ranks(row, msk, hold, w, ct, first, last):
            scan(V(hold, 0, w), V("kf", 0, w), V(msk, 0, w), 0.0, A.min, A.max)
            stride = 896 if ct == "ct1" else 512
            for m in range(w // 16):
                at, s = stride * (m // 4) + m % 4, col(hold, 16 * m + 15)
                if m < first:
                    d = V("dg", 224 * m, 224 * m + w)
                    act(d, V(row, 0, w), F.Sign, bias=s, scale=-1.0)
                    if m:
                        act(V(ct, at, at + 64 * m, 4), V("dg", 224 * m, 224 * m + 16 * m), F.Sign, bias=-0.5, scale=-1.0)
                    act(V(ct, at + 64 * m, at + 4 * w - m % 4, 4), V("dg", 224 * m + 16 * m, 224 * m + w), F.Sign, bias=0.5, scale=-1.0)
                else:
                    if m:
                        ts(V(ct, at, at + 64 * m, 4), V(row, 0, 16 * m), s, A.is_gt)
                    ts(V(ct, at + 64 * m, at + 4 * w - m % 4, 4), V(row, 16 * m, w), s, A.is_ge)
            tt(V(ct, stride * last + 2, stride * last + 4 * w, 4), G(hold, 0, w, V("co", 40, 40 + w // 16)), V(msk, 0, w), A.is_equal)

        tt(V("pm", 0, N), V(c, 0, n, 2), V(c, 1, n, 2), A.min)
        tt(V("b1", 0, N), V("pm", 0, N), V("mk", 0, N), A.min)
        ranks("pm", "b1", "h1", N, "ct1", 6, 3)
        for k, u in enumerate([2, 3, 0, 1]):
            qz("qc1", "sc1", 224 * u, 224 * u + N, V("ct1", 896 * u, 896 * u + 4 * N))
            mm(5, "qb", "sb", [128, 384, 0, 256][u], "qc1", "sc1", 224 * u, 224 * u + N, k == 0, k == 3)
        ts(V("m1", 0, N), V("ps", 2560, 2560 + N), 15.5, A.is_lt)
        scan(V("px", 0, N), V("m1", 0, N), V("m1", 0, N), 0.0, A.add, A.max)
        for m in range(8):
            if m < 5:
                act(V("junk", 4096 + 224 * m, 4096 + 224 * m + N), V("px", 0, N), F.Sign, bias=col("cw", 32 + m), scale=-1.0, acc=col("a1", m))
            else:
                a = 232 * (m - 5)
                ts(V("pv", a, a + N), V("px", 0, N), col("cw", 32 + m), A.is_lt, 2.0, A.mult)
                red(col("a1", m), V("pv", a, a + N + 1))
        ts(V("l2", 0, 8), V("a1", 0, 8), col("cst", 4 + t), A.add)
        l2 = V("l2", 0, 8)
        act(V("r2", 0, 128), G(c, 0, n, l2), F.Copy)
        tt(V("b2", 0, 128), G(c, 0, n, l2), V("mk", 0, 128), A.min)
        act(V("x2", 0, 128), G("iom", 0, 512, l2), F.Copy, scale=1.0 / 512)
        ranks("r2", "b2", "h2", 128, "ct2", 4, 2)
        for k, u in enumerate([1, 2, 0]):
            qz("qc2", "sc2", 128 * u, 128 * u + 128, V("ct2", 512 * u, 512 * u + 512))
            mm(6, "qb", "sb", [128, 0, 256][u], "qc2", "sc2", 128 * u, 128 * u + 128, k == 0, k == 2)
        tt(V("w2", 0, 128), V("ps", 3072, 3200), V("x2", 0, 128), A.add)
        for m in range(4):
            ts(V("cl", 132 * m, 132 * m + 128), V("w2", 0, 128), col("cw", 40 + m), A.max, col("cw", 44 + m), A.min)
        for m in range(4):
            if m < 3:
                act(V("jf", 132 * m, 132 * m + 129), V("cl", 132 * m, 132 * m + 129), F.Copy, acc=col("a2", m))
            else:
                red(col("a2", m), V("cl", 132 * m, 132 * m + 129))
        ts(V("eo%d" % t, 0, 4), V("a2", 0, 4), 512.0, A.mult)
        ei = V("ei%d" % t, 0, 4)
        remote([(ei, V("eo%d" % t, 0, 4), False)], "ae%d" % t, 1024)
        for b in range(4):
            h, w = V(xt, 4 * n + b, 4 * n + 256, 4), G("dp", 448 * b, 448 * b + n, ei)
            if b < 2:
                cp(h, w)
            else:
                act(h, w, F.Copy)
        qz("qh", "sh", 0, 128, V(xt, 4 * n - 256, 4 * n + 256))
        mm(7, "qp", "sp", 0, "qh", "sh", 0, 128)
        for b in range(4):
            act(V("xh", 512 * b + n, 512 * b + n + 64), V(xt, 4 * n + b, 4 * n + 256, 4), F.Copy, scale=0.5)
            act(V("xg", 512 * b + n, 512 * b + n + 64), V(xt, 4 * n + b, 4 * n + 256, 4), F.Copy, scale=0.5)
        w256 = lambda b: V(b, 0, 256)
        for a in range(4):
            tt(V("de", a, 256, 4), V("ps", 3584 + 64, 3584 + 128), V("sn", a, 256, 4), A.subtract)
        act(w256("ga"), w256("de"), F.Abs)
        act(w256("gs"), G("de", 0, 256, so(0)), F.Abs)
        tt(w256("cs"), G(c, 0, n, no), w256("ga"), A.max)
        scan(w256("dm"), w256("k4"), w256("cs"), 0.0, A.max, A.min)
        for a in range(1, 4):
            tt(V("ge", a, 256, 4), V("cs", a, 256, 4), V("dm", a - 1, 256, 4), A.is_ge)
        scan(w256("pq"), w256("ge"), V("dq", 256 * t, 256 * t + 256), 0.0, A.mult, A.max)
        cp(V("pi", 0, 64), V("pq", 3, 256, 4))
        ts(V("pi", 64, 128), V("pi", 0, 64), 511, A.bitwise_and)
        cp(V("pf", n, n + 64), V("pi", 64, 128))
        tt(w256("pr"), G("dm", 0, 256, so(1)), w256("gs"), A.max)
        scan(w256("s1"), V("ks", ks, ks + 256), w256("pr"), BIG, A.max, A.min)
        tt(w256("ne"), w256("pr"), w256("s1"), A.not_equal)
        tt(w256("mv"), G(c, 0, n, so(2)), w256("pr"), A.is_gt)
        tt(w256("d1"), w256("mv"), ak, A.mult)
        tt(w256("d2"), G("pf", 0, n, so(2)), w256("d1"), A.max)
        scan(w256("s2"), w256("ne"), w256("d2"), 0.0, A.mult, A.max)
        cp(G("pf", 0, 768, so(3)), w256("s2"))
        n2 = n + NEW
        lp = 0 if t == 0 else 288
        wrap(V("lv", lp, lp + n2 // 16), "pf", 0, n2, 1)
        if t == 1:
            for k in range(8):
                dma("s", lambda k=k: T.op[k:k + 1, :], lambda k=k: T.pf[16 * k:16 * k + 1, 0:512], [V("pf", 0, 512)], [], 0)
        h = n2 // 2
        qn, sn = "qx%d" % (t + 1), "sx%d" % (t + 1)
        for k in range(2):
            a, e = k * h, k * h + h
            for b in range(4):
                tt(V("yt", 4 * a + b, 4 * e, 4), G("xh", 512 * b, 512 * b + n2, V("lv", lp + a // 16, lp + e // 16)), V("xg", 512 * b + a, 512 * b + e), A.add)
            qz("qy", "sy", a, e, V("yt", 4 * a, 4 * e))
            for b in range(4):
                mm(4 * k + b, "qw", "sw", 128 * b, "qy", "sy", a, e)
        for k in range(2):
            for b in range(4):
                act(V("rb", 512 * b + k * h, 512 * b + k * h + h), V("ps", 512 * (4 * k + b), 512 * (4 * k + b) + h), F.Relu, scale=0.03125)
        for k, (a, e) in enumerate([(0, h), (h, n2)] if t == 0 else [(0, h), (h, h + 128), (h + 128, n2)]):
            for b in range(4):
                tt(V(xn, 4 * a + b, 4 * e, 4), V("rb", 512 * b + a, 512 * b + e), V(xt, 4 * a + b, 4 * e, 4), A.add)
            qz(qn, sn, a, e, V(xn, 4 * a, 4 * e))
            if t == 1:
                mm(k, "qv", "sv", 0, qn, sn, a, e)
                act(V("yo", a, e), V("ps", 512 * k, 512 * k + e - a), F.Copy)
                dma("s", lambda a=a, e=e: T.oc[:, 4 * a:4 * e], lambda a=a, e=e: T.qx2[:, a:e].bitcast(dt.uint8), [V(qn, a, e)], [], 512 * (e - a))
                dma("a", lambda a=a, e=e: T.y[:, a:e], lambda a=a, e=e: T.yo[:, a:e], [V("yo", a, e)], [], 512 * (e - a))
    for k in range(4):
        dma("sa"[k % 2], lambda k=k: T.osc[4 * k:4 * k + 4, :], lambda k=k: T.sx2[32 * k:32 * k + 4, 0:512], [V("sx2", 0, 512)], [], 0)
    return ops, 6 * n_out


def depend(ops):
    seen = {}
    for i, o in enumerate(ops):
        d = set()
        acc = [(v[0], _bits(v), False) for v in o["rd"]] + [(v[0], _bits(v), True) for v in o["wr"]]
        for b, m, w in acc:
            for j, m2, w2 in seen.get(b, []):
                if m & m2 and (w or w2 or (b == "ps" and ops[j]["q"] != o["q"])):
                    if not (o["acc"] and b == "ps" and ops[j]["q"] == "t"):
                        d.add(j)
        o["order"] = set(j for b, m, w in acc if b == "ps" and o["acc"] for j, m2, w2 in seen.get(b, []) if m & m2 and ops[j]["q"] == "t")
        o["dep"] = d
        for b, m, w in acc:
            if w and not o["acc"]:
                seen[b] = [x for x in seen.get(b, []) if x[1] & ~m]
            seen.setdefault(b, []).append((i, m, w))


def place(ops, prio, pred, back):
    n = len(ops)
    start, end, busy = [0.0] * n, [0.0] * n, {q: [] for q in "vatsg"}
    for i in sorted(range(n), key=lambda i: -prio[i]):
        q, c, lat = ops[i]
        t = 0.0
        for j, w in pred[i]:
            if end[j] + w > t:
                t = end[j] + w
        if back:
            t += lat
        if q != "n":
            row = busy[q]
            k, hi = 0, len(row)
            while k < hi:
                mid = (k + hi) // 2
                if row[mid][0] < t:
                    k = mid + 1
                else:
                    hi = mid
            if k and row[k - 1][1] > t:
                t = row[k - 1][1]
            while k < len(row) and t + c > row[k][0]:
                t = row[k][1]
                k += 1
            row.insert(k, (t, t + c))
        start[i], end[i] = t, t + c + (0.0 if back else lat)
    return max(end), start, end


def schedule(ops):
    n = len(ops)
    pred = [[(j, WAKE) for j in o["dep"]] + [(j, 0.0) for j in o["order"]] for o in ops]
    succ = [[] for o in ops]
    for i in range(n):
        for j, w in pred[i]:
            succ[j].append((i, w))
    ops = [(o["q"], o["cost"], o["lat"]) for o in ops]
    prio = [0.0] * n
    for i in range(n - 1, -1, -1):
        prio[i] = max([prio[j] + w for j, w in succ[i]] + [0.0]) + ops[i][1] + ops[i][2]
    now = best = place(ops, prio, pred, False)
    x = SEED
    for turn in range(TURNS):
        p = [-s for s in now[1]]
        for k in range(25):
            x = (x * 1103515245 + 12345) % 2147483648
            i = (x >> 8) % n
            x = (x * 1103515245 + 12345) % 2147483648
            p[i] += ((x >> 8) / 4194304.0 - 1) ** 3 * 4500
        for i in range(n - 1, -1, -1):
            for j, w in pred[i]:
                if p[j] <= p[i]:
                    p[j] = p[i] + 1
        one = place(ops, p, pred, False)
        two = place(ops, place(ops, one[2], succ, True)[2], pred, False)
        if two[0] < one[0]:
            one = two
        if one[0] <= now[0] + 60.0 * (1 - turn / TURNS):
            now = one
        if one[0] < best[0]:
            best = one
    PLAN["time"] = best[0]
    return sorted(range(n), key=lambda i: (best[1][i], i))


PLAN = {}
SEED, TURNS = 2, 9000


def rank_program(g, core, T, topo):
    rank = T.rank_of(core)
    if rank is None:
        return
    ops, sent = collect(g, core, T, topo, rank)
    depend(ops)
    if "order" not in PLAN:
        PLAN["order"] = schedule(ops)
    order = list(PLAN["order"])
    ops.append({"q": "s", "kind": "end", "dep": set(i for i, o in enumerate(ops) if o["kind"] == "d" and not o["wr"])})
    order.append(len(ops) - 1)
    known, before, group, groups, waits = {}, {}, {}, [], {}
    last, count = [0] * NS, [0] * NS
    pos = {j: p for p, j in enumerate(order)}
    for i in order:
        o = ops[i]
        if o["kind"] == "n":
            continue
        k, w = known.get(o["q"], 0), []
        fresh = {}
        for j in sorted(o["dep"], key=lambda j: -pos[j]):
            if k >> j & 1:
                continue
            if ops[j]["kind"] == "n":
                w.append(ops[j]["sem"])
                k |= 1 << j
            elif j in group:
                w.append(group[j])
                k |= groups[group[j]][2]
            else:
                fresh.setdefault(ops[j]["kind"], []).append(j)
                k |= before[j] | 1 << j
        for kind, js in fresh.items():
            bits = 0
            for j in js:
                group[j] = len(groups)
                bits |= before[j] | 1 << j
            w.append(len(groups))
            groups.append((kind, js, bits))
        known[o["q"]], before[i], waits[i] = k, k, w
    name = {}
    for x in sorted(range(len(groups)), key=lambda x: min(pos[j] for j in groups[x][1])):
        kind, js, bits = groups[x]
        common = -1
        for j in js:
            common &= before[j]
        lo, hi = (0, 16) if kind == "d" else (16, NS)
        s = [s for s in range(lo, hi) if last[s] & ~common == 0][0]
        count[s] += len(js) * (16 if kind == "d" else 1)
        last[s] = sum(1 << j for j in js)
        name[x] = ("w%d" % s, count[s])
    queue = {"v": g.vector, "a": g.scalar, "t": g.tensor, "s": g.sync, "g": g}
    for i in order:
        o = ops[i]
        if o["kind"] == "n":
            continue
        for x in waits[i]:
            s, c = x if isinstance(x, tuple) else name[x]
            queue[o["q"]].wait_ge(T.sem[s], c)
        if o["kind"] != "end":
            x = o["fn"]()
            if i in group:
                x.then_inc(T.sem[name[group[i]][0]], 16 if o["kind"] == "d" else 1)
    g.wait_ge(T.sem.sent, sent)
